import numpy as np, ml_dtypes
CORES = [6,14,22,30,134,142,150,158,262,270,278,286,390,398,406,414]
N = 16
GROUPS = [[0,4,8,12],[1,5,9,13],[2,6,10,14],[3,7,11,15]]
def setup_inputs(rng):
    return {"x": rng.standard_normal((N, 128, 256), dtype=np.float32).astype(ml_dtypes.bfloat16)}
def reference(x):
    y = np.empty((N, 128, 1024), x.dtype)
    for g in GROUPS:
        s = np.concatenate([x[r] for r in g], axis=1)
        for r in g:
            y[r] = s
    return {"y": y}

@@ -1,0 +1,84 @@
+from concourse.bass import DstId, RemoteDMATransfer
+
+RANK_CORE = 6
+HC_CORE = 4
+HS_CORE = 2
+
+SCRATCH = {
+    "stage": ("dram", [2, 128, 128], "bfloat16"),
+    "land": ("dram", [6, 128, 128], "bfloat16"),
+}
+SEMAPHORES = ["loaded", "sent", "stored", "relay_in", "a0", "a1", "a2", "a3", "a4", "a5"]
+
+SWITCH_ENG, CABLE_ENG = 0x000F, 0x00F0
+OFF_CHIP_ENG, ON_CHIP_ENG = 0x00FF, 0xFF00
+
+
+def rank_program(g, core, T, topo):
+    S = T.sem
+    rank = T.rank_of(core - core % 8 + RANK_CORE)
+    role = core % 8
+    if rank is None or role not in (RANK_CORE, HC_CORE, HS_CORE):
+        return
+    group = [grp for grp in T.tables["GROUPS"] if rank in grp][0]
+    at_host = {}
+    for place, member in enumerate(group):
+        at_host[topo.host(T.cores[member])] = (T.cores[member], place)
+    h = topo.host(core)
+    ns, nc = h ^ 1, 3 - h
+    diag = 3 - ns
+
+    def on_chip_of(hst, which):
+        return at_host[hst][0] - RANK_CORE + which
+
+    def xfer(dst_core, src_ap, dst_ap, mask, sem):
+        rid, pid = topo.addr(dst_core, core)
+        return RemoteDMATransfer(dst_ids=[DstId(rid=rid, pnc=pid)], dma_engine_mask=mask, remote_sem=sem,
+                                 src=src_ap, dst=dst_ap)
+
+    if role == HC_CORE:
+        g.wait_ge(S.relay_in, 4)
+        g.remote_dma_fused([xfer(on_chip_of(nc, RANK_CORE), T.stage[0], T.land[4], OFF_CHIP_ENG, S.a4),
+                            xfer(on_chip_of(h, RANK_CORE), T.stage[0], T.land[0], ON_CHIP_ENG, S.a0)], local_sem=S.sent)
+        g.wait_ge(S.sent, 16)
+        return
+    if role == HS_CORE:
+        g.wait_ge(S.relay_in, 4)
+        g.remote_dma_fused([xfer(on_chip_of(ns, RANK_CORE), T.stage[0], T.land[5], OFF_CHIP_ENG, S.a5),
+                            xfer(on_chip_of(h, RANK_CORE), T.stage[0], T.land[3], ON_CHIP_ENG, S.a3)], local_sem=S.sent)
+        g.wait_ge(S.sent, 16)
+        return
+
+    w = T.x.shape[1]
+
+    def y_half(hst, half):
+        place = at_host[hst][1]
+        return T.y[64 * half:64 * half + 64, place * w:(place + 1) * w]
+
+    g.sync.dma_start(T.stage[:], T.x[:]).then_inc(S.loaded, 16)
+    g.wait_ge(S.loaded, 16)
+    g.remote_dma_fused([xfer(on_chip_of(ns, HC_CORE), T.stage[0], T.stage[0], SWITCH_ENG, S.relay_in),
+                        xfer(on_chip_of(nc, HS_CORE), T.stage[1], T.stage[0], CABLE_ENG, S.relay_in)], local_sem=S.sent)
+    g.remote_dma_fused([xfer(on_chip_of(ns, RANK_CORE), T.stage[1], T.land[1], SWITCH_ENG, S.a1),
+                        xfer(on_chip_of(nc, RANK_CORE), T.stage[0], T.land[2], CABLE_ENG, S.a2)], local_sem=S.sent)
+
+    q = g.sync
+    q.wait_ge(S.a1, 4)
+    q.dma_start(y_half(ns, 1), T.land[1]).then_inc(S.stored, 16)
+    q.wait_ge(S.a0, 8)
+    q.dma_start(y_half(ns, 0), T.land[0]).then_inc(S.stored, 16)
+    q.wait_ge(S.a4, 8)
+    q.dma_start(y_half(diag, 0), T.land[4]).then_inc(S.stored, 16)
+
+    q = g.scalar
+    q.wait_ge(S.sent, 16)
+    q.dma_start(T.y[:, at_host[h][1] * w:(at_host[h][1] + 1) * w], T.x[:]).then_inc(S.stored, 16)
+    q.wait_ge(S.a2, 4)
+    q.dma_start(y_half(nc, 0), T.land[2]).then_inc(S.stored, 16)
+    q.wait_ge(S.a3, 8)
+    q.dma_start(y_half(nc, 1), T.land[3]).then_inc(S.stored, 16)
+    q.wait_ge(S.a5, 8)
+    q.dma_start(y_half(diag, 1), T.land[5]).then_inc(S.stored, 16)
+
+    g.wait_ge(S.sent, 16)
+    g.wait_ge(S.stored, 16 * 7)

@@ -1,24 +1,22 @@
 from concourse.bass import DstId, RemoteDMATransfer
 
 RANK_CORE = 6
-HC_CORE = 4
-HS_CORE = 2
+HC = (4, 2)
+HS = (7, 1)
+XC = (0, 5)
 
 SCRATCH = {
-    "stage": ("dram", [2, 128, 128], "bfloat16"),
-    "land": ("dram", [6, 128, 128], "bfloat16"),
+    "stage": ("dram", [4, 128, 64], "bfloat16"),
+    "land": ("dram", [12, 128, 64], "bfloat16"),
 }
-SEMAPHORES = ["loaded", "sent", "stored", "relay_in", "a0", "a1", "a2", "a3", "a4", "a5"]
-
-SWITCH_ENG, CABLE_ENG = 0x000F, 0x00F0
-OFF_CHIP_ENG, ON_CHIP_ENG = 0x00FF, 0xFF00
+SEMAPHORES = ["loaded", "sent", "stored", "own", "relay_in", "a0", "a1", "a2", "a3", "a4", "a5"]
 
 
 def rank_program(g, core, T, topo):
     S = T.sem
     rank = T.rank_of(core - core % 8 + RANK_CORE)
     role = core % 8
-    if rank is None or role not in (RANK_CORE, HC_CORE, HS_CORE):
+    if rank is None or role not in (RANK_CORE,) + HC + HS + XC:
         return
     group = [grp for grp in T.tables["GROUPS"] if rank in grp][0]
     at_host = {}
@@ -36,49 +34,55 @@ def rank_program(g, core, T, topo):
         return RemoteDMATransfer(dst_ids=[DstId(rid=rid, pnc=pid)], dma_engine_mask=mask, remote_sem=sem,
                                  src=src_ap, dst=dst_ap)
 
-    if role == HC_CORE:
+    if role in XC:
+        q = XC.index(role)
+        rid, pid = topo.addr(on_chip_of(nc, RANK_CORE), core)
         g.wait_ge(S.relay_in, 4)
-        g.remote_dma_fused([xfer(on_chip_of(nc, RANK_CORE), T.stage[0], T.land[4], OFF_CHIP_ENG, S.a4),
-                            xfer(on_chip_of(h, RANK_CORE), T.stage[0], T.land[0], ON_CHIP_ENG, S.a0)], local_sem=S.sent)
-        g.wait_ge(S.sent, 16)
+        g.remote_dma(T.land[4 + q], T.stage[0], S.a2, S.sent, pid, rid, 0x00FF)
+        g.wait_ge(S.sent, 8)
         return
-    if role == HS_CORE:
-        g.wait_ge(S.relay_in, 4)
-        g.remote_dma_fused([xfer(on_chip_of(ns, RANK_CORE), T.stage[0], T.land[5], OFF_CHIP_ENG, S.a5),
-                            xfer(on_chip_of(h, RANK_CORE), T.stage[0], T.land[3], ON_CHIP_ENG, S.a3)], local_sem=S.sent)
+    if role != RANK_CORE:
+        if role in HC:
+            q = HC.index(role)
+            far, far_sem, near_slot, near_sem = nc, S.a4, q, S.a0
+        else:
+            q = 2 + HS.index(role)
+            far, far_sem, near_slot, near_sem = ns, S.a5, 4 + q, S.a3
+        g.wait_ge(S.relay_in, 2)
+        g.remote_dma_fused([xfer(on_chip_of(far, RANK_CORE), T.stage[0], T.land[8 + q], 0x00FF, far_sem),
+                            xfer(on_chip_of(h, RANK_CORE), T.stage[0], T.land[near_slot], 0xFF00, near_sem)],
+                           local_sem=S.sent)
         g.wait_ge(S.sent, 16)
         return
 
     w = T.x.shape[1]
 
-    def y_half(hst, half):
+    def store(queue, sem, count, s, hst, half):
         place = at_host[hst][1]
-        return T.y[64 * half:64 * half + 64, place * w:(place + 1) * w]
+        queue.wait_ge(sem, count)
+        queue.dma_start(T.y[64 * half:64 * half + 64, place * w:(place + 1) * w],
+                        T.land[4 * s + 2 * half:4 * s + 2 * half + 2]).then_inc(S.stored, 16)
 
     g.sync.dma_start(T.stage[:], T.x[:]).then_inc(S.loaded, 16)
     g.wait_ge(S.loaded, 16)
-    g.remote_dma_fused([xfer(on_chip_of(ns, HC_CORE), T.stage[0], T.stage[0], SWITCH_ENG, S.relay_in),
-                        xfer(on_chip_of(nc, HS_CORE), T.stage[1], T.stage[0], CABLE_ENG, S.relay_in)], local_sem=S.sent)
-    g.remote_dma_fused([xfer(on_chip_of(ns, RANK_CORE), T.stage[1], T.land[1], SWITCH_ENG, S.a1),
-                        xfer(on_chip_of(nc, RANK_CORE), T.stage[0], T.land[2], CABLE_ENG, S.a2)], local_sem=S.sent)
+    g.remote_dma_fused([xfer(on_chip_of(nc, HS[0]), T.stage[2], T.stage[0], 0x0030, S.relay_in),
+                        xfer(on_chip_of(nc, HS[1]), T.stage[3], T.stage[0], 0x00C0, S.relay_in),
+                        xfer(on_chip_of(ns, HC[0]), T.stage[0], T.stage[0], 0x0003, S.relay_in),
+                        xfer(on_chip_of(ns, HC[1]), T.stage[1], T.stage[0], 0x000C, S.relay_in),
+                        xfer(on_chip_of(h, XC[0]), T.stage[0], T.stage[0], 0x0F00, S.relay_in),
+                        xfer(on_chip_of(h, XC[1]), T.stage[1], T.stage[0], 0xF000, S.relay_in)], local_sem=S.sent)
+    g.remote_dma_fused([xfer(on_chip_of(ns, RANK_CORE), T.stage[2], T.land[2], 0x0003, S.a1),
+                        xfer(on_chip_of(ns, RANK_CORE), T.stage[3], T.land[3], 0x000C, S.a1)], local_sem=S.sent)
+    g.dma_start(T.y[:, at_host[h][1] * w:(at_host[h][1] + 1) * w], T.x[:]).then_inc(S.own, 16)
 
-    q = g.sync
-    q.wait_ge(S.a1, 4)
-    q.dma_start(y_half(ns, 1), T.land[1]).then_inc(S.stored, 16)
-    q.wait_ge(S.a0, 8)
-    q.dma_start(y_half(ns, 0), T.land[0]).then_inc(S.stored, 16)
-    q.wait_ge(S.a4, 8)
-    q.dma_start(y_half(diag, 0), T.land[4]).then_inc(S.stored, 16)
+    store(g.sync, S.a1, 4, 0, ns, 1)
+    store(g.sync, S.a0, 16, 0, ns, 0)
+    store(g.sync, S.a4, 16, 2, diag, 0)
 
-    q = g.scalar
-    q.wait_ge(S.sent, 16)
-    q.dma_start(T.y[:, at_host[h][1] * w:(at_host[h][1] + 1) * w], T.x[:]).then_inc(S.stored, 16)
-    q.wait_ge(S.a2, 4)
-    q.dma_start(y_half(nc, 0), T.land[2]).then_inc(S.stored, 16)
-    q.wait_ge(S.a3, 8)
-    q.dma_start(y_half(nc, 1), T.land[3]).then_inc(S.stored, 16)
-    q.wait_ge(S.a5, 8)
-    q.dma_start(y_half(diag, 1), T.land[5]).then_inc(S.stored, 16)
+    store(g.scalar, S.a2, 16, 1, nc, 0)
+    store(g.scalar, S.a3, 16, 1, nc, 1)
+    store(g.scalar, S.a5, 16, 2, diag, 1)
 
-    g.wait_ge(S.sent, 16)
-    g.wait_ge(S.stored, 16 * 7)
+    g.wait_ge(S.own, 16)
+    g.wait_ge(S.sent, 20)
+    g.wait_ge(S.stored, 16 * 6)

@@ -1,22 +1,24 @@
 from concourse.bass import DstId, RemoteDMATransfer
 
 RANK_CORE = 6
-HC = (4, 2)
-HS = (7, 1)
-XC = (0, 5)
+HCA, HCB = 4, 2
+HS = 1
+XC = 0
+ROWS = {"a": (0, 48), "b": (48, 80), "c": (80, 128)}
 
 SCRATCH = {
-    "stage": ("dram", [4, 128, 64], "bfloat16"),
-    "land": ("dram", [12, 128, 64], "bfloat16"),
+    "sa": ("dram", [128, 96], "bfloat16"), "sb": ("dram", [128, 64], "bfloat16"), "sc": ("dram", [128, 96], "bfloat16"),
+    "la": ("dram", [3, 128, 96], "bfloat16"), "lb": ("dram", [3, 128, 64], "bfloat16"), "lc": ("dram", [3, 128, 96], "bfloat16"),
 }
-SEMAPHORES = ["loaded", "sent", "stored", "own", "relay_in", "a0", "a1", "a2", "a3", "a4", "a5"]
+SEMAPHORES = ["loaded", "loaded_b", "sent", "stored", "own", "relay_in",
+              "a0", "a1", "a2", "b0", "b1", "b2", "c0", "c1", "c2"]
 
 
 def rank_program(g, core, T, topo):
     S = T.sem
     rank = T.rank_of(core - core % 8 + RANK_CORE)
     role = core % 8
-    if rank is None or role not in (RANK_CORE,) + HC + HS + XC:
+    if rank is None or role not in (RANK_CORE, HCA, HCB, HS, XC):
         return
     group = [grp for grp in T.tables["GROUPS"] if rank in grp][0]
     at_host = {}
@@ -34,55 +36,57 @@ def rank_program(g, core, T, topo):
         return RemoteDMATransfer(dst_ids=[DstId(rid=rid, pnc=pid)], dma_engine_mask=mask, remote_sem=sem,
                                  src=src_ap, dst=dst_ap)
 
-    if role in XC:
-        q = XC.index(role)
+    if role == XC:
         rid, pid = topo.addr(on_chip_of(nc, RANK_CORE), core)
-        g.wait_ge(S.relay_in, 4)
-        g.remote_dma(T.land[4 + q], T.stage[0], S.a2, S.sent, pid, rid, 0x00FF)
+        g.wait_ge(S.relay_in, 8)
+        g.remote_dma(T.la[1], T.sa[:], S.a1, S.sent, pid, rid, 0x00FF)
         g.wait_ge(S.sent, 8)
         return
     if role != RANK_CORE:
-        if role in HC:
-            q = HC.index(role)
-            far, far_sem, near_slot, near_sem = nc, S.a4, q, S.a0
-        else:
-            q = 2 + HS.index(role)
-            far, far_sem, near_slot, near_sem = ns, S.a5, 4 + q, S.a3
-        g.wait_ge(S.relay_in, 2)
-        g.remote_dma_fused([xfer(on_chip_of(far, RANK_CORE), T.stage[0], T.land[8 + q], 0x00FF, far_sem),
-                            xfer(on_chip_of(h, RANK_CORE), T.stage[0], T.land[near_slot], 0xFF00, near_sem)],
-                           local_sem=S.sent)
+        buf, land, far, far_sem, near, near_sem = {
+            HCA: (T.sa, T.la, nc, S.a2, 0, S.a0),
+            HCB: (T.sb, T.lb, nc, S.b2, 0, S.b0),
+            HS: (T.sc, T.lc, ns, S.c2, 1, S.c1)}[role]
+        g.wait_ge(S.relay_in, 4)
+        g.remote_dma_fused([xfer(on_chip_of(far, RANK_CORE), buf[:], land[2], 0x00FF, far_sem),
+                            xfer(on_chip_of(h, RANK_CORE), buf[:], land[near], 0xFF00, near_sem)], local_sem=S.sent)
         g.wait_ge(S.sent, 16)
         return
 
     w = T.x.shape[1]
+    src_host = (ns, nc, diag)
 
-    def store(queue, sem, count, s, hst, half):
-        place = at_host[hst][1]
-        queue.wait_ge(sem, count)
-        queue.dma_start(T.y[64 * half:64 * half + 64, place * w:(place + 1) * w],
-                        T.land[4 * s + 2 * half:4 * s + 2 * half + 2]).then_inc(S.stored, 16)
+    def store(queue, piece, s, count):
+        lo, hi = ROWS[piece]
+        place = at_host[src_host[s]][1]
+        queue.wait_ge(S["%s%d" % (piece, s)], count)
+        queue.dma_start(T.y[lo:hi, place * w:(place + 1) * w], T["l" + piece][s]).then_inc(S.stored, 16)
 
-    g.sync.dma_start(T.stage[:], T.x[:]).then_inc(S.loaded, 16)
-    g.wait_ge(S.loaded, 16)
-    g.remote_dma_fused([xfer(on_chip_of(nc, HS[0]), T.stage[2], T.stage[0], 0x0030, S.relay_in),
-                        xfer(on_chip_of(nc, HS[1]), T.stage[3], T.stage[0], 0x00C0, S.relay_in),
-                        xfer(on_chip_of(ns, HC[0]), T.stage[0], T.stage[0], 0x0003, S.relay_in),
-                        xfer(on_chip_of(ns, HC[1]), T.stage[1], T.stage[0], 0x000C, S.relay_in),
-                        xfer(on_chip_of(h, XC[0]), T.stage[0], T.stage[0], 0x0F00, S.relay_in),
-                        xfer(on_chip_of(h, XC[1]), T.stage[1], T.stage[0], 0xF000, S.relay_in)], local_sem=S.sent)
-    g.remote_dma_fused([xfer(on_chip_of(ns, RANK_CORE), T.stage[2], T.land[2], 0x0003, S.a1),
-                        xfer(on_chip_of(ns, RANK_CORE), T.stage[3], T.land[3], 0x000C, S.a1)], local_sem=S.sent)
+    g.sync.dma_start(T.sc[:], T.x[80:128, :]).then_inc(S.loaded, 16)
+    g.scalar.dma_start(T.sa[:], T.x[0:48, :]).then_inc(S.loaded, 16)
+    g.sync.dma_start(T.sb[:], T.x[48:80, :]).then_inc(S.loaded_b, 16)
+    g.wait_ge(S.loaded, 32)
+    g.remote_dma_fused([xfer(on_chip_of(nc, HS), T.sc[:], T.sc[:], 0x00F0, S.relay_in),
+                        xfer(on_chip_of(ns, HCA), T.sa[:], T.sa[:], 0x000F, S.relay_in),
+                        xfer(on_chip_of(h, XC), T.sa[:], T.sa[:], 0xFF00, S.relay_in)], local_sem=S.sent)
+    g.wait_ge(S.loaded_b, 16)
+    g.remote_dma_fused([xfer(on_chip_of(ns, HCB), T.sb[:], T.sb[:], 0x000F, S.relay_in),
+                        xfer(on_chip_of(nc, RANK_CORE), T.sb[:], T.lb[1], 0x00F0, S.b1)], local_sem=S.sent)
+    rid, pid = topo.addr(on_chip_of(ns, RANK_CORE), core)
+    g.remote_dma(T.lc[0], T.sc[:], S.c0, S.sent, pid, rid, 0x000F)
     g.dma_start(T.y[:, at_host[h][1] * w:(at_host[h][1] + 1) * w], T.x[:]).then_inc(S.own, 16)
 
-    store(g.sync, S.a1, 4, 0, ns, 1)
-    store(g.sync, S.a0, 16, 0, ns, 0)
-    store(g.sync, S.a4, 16, 2, diag, 0)
+    store(g.sync, "c", 0, 4)
+    store(g.sync, "a", 0, 8)
+    store(g.sync, "b", 2, 8)
+    store(g.sync, "a", 1, 8)
+    store(g.sync, "a", 2, 8)
 
-    store(g.scalar, S.a2, 16, 1, nc, 0)
-    store(g.scalar, S.a3, 16, 1, nc, 1)
-    store(g.scalar, S.a5, 16, 2, diag, 1)
+    store(g.scalar, "b", 0, 8)
+    store(g.scalar, "b", 1, 4)
+    store(g.scalar, "c", 1, 8)
+    store(g.scalar, "c", 2, 8)
 
     g.wait_ge(S.own, 16)
-    g.wait_ge(S.sent, 20)
-    g.wait_ge(S.stored, 16 * 6)
+    g.wait_ge(S.sent, 28)
+    g.wait_ge(S.stored, 16 * 9)

from concourse.bass import DstId, RemoteDMATransfer

RANK_CORE = 6
HCA, HCB = 4, 2
HS = 1
XC = 0
ROWS = {"a": (0, 48), "b": (48, 80), "c": (80, 128)}

SCRATCH = {
    "sa": ("dram", [128, 96], "bfloat16"), "sb": ("dram", [128, 64], "bfloat16"), "sc": ("dram", [128, 96], "bfloat16"),
    "la": ("dram", [3, 128, 96], "bfloat16"), "lb": ("dram", [3, 128, 64], "bfloat16"), "lc": ("dram", [3, 128, 96], "bfloat16"),
}
SEMAPHORES = ["loaded", "loaded_b", "sent", "stored", "own", "relay_in",
              "a0", "a1", "a2", "b0", "b1", "b2", "c0", "c1", "c2"]


def rank_program(g, core, T, topo):
    S = T.sem
    rank = T.rank_of(core - core % 8 + RANK_CORE)
    role = core % 8
    if rank is None or role not in (RANK_CORE, HCA, HCB, HS, XC):
        return
    group = [grp for grp in T.tables["GROUPS"] if rank in grp][0]
    at_host = {}
    for place, member in enumerate(group):
        at_host[topo.host(T.cores[member])] = (T.cores[member], place)
    h = topo.host(core)
    ns, nc = h ^ 1, 3 - h
    diag = 3 - ns

    def on_chip_of(hst, which):
        return at_host[hst][0] - RANK_CORE + which

    def xfer(dst_core, src_ap, dst_ap, mask, sem):
        rid, pid = topo.addr(dst_core, core)
        return RemoteDMATransfer(dst_ids=[DstId(rid=rid, pnc=pid)], dma_engine_mask=mask, remote_sem=sem,
                                 src=src_ap, dst=dst_ap)

    if role == XC:
        rid, pid = topo.addr(on_chip_of(nc, RANK_CORE), core)
        g.wait_ge(S.relay_in, 8)
        g.remote_dma(T.la[1], T.sa[:], S.a1, S.sent, pid, rid, 0x00FF)
        g.wait_ge(S.sent, 8)
        return
    if role != RANK_CORE:
        buf, land, far, far_sem, near, near_sem = {
            HCA: (T.sa, T.la, nc, S.a2, 0, S.a0),
            HCB: (T.sb, T.lb, nc, S.b2, 0, S.b0),
            HS: (T.sc, T.lc, ns, S.c2, 1, S.c1)}[role]
        g.wait_ge(S.relay_in, 4)
        g.remote_dma_fused([xfer(on_chip_of(far, RANK_CORE), buf[:], land[2], 0x00FF, far_sem),
                            xfer(on_chip_of(h, RANK_CORE), buf[:], land[near], 0xFF00, near_sem)], local_sem=S.sent)
        g.wait_ge(S.sent, 16)
        return

    w = T.x.shape[1]
    src_host = (ns, nc, diag)

    def store(queue, piece, s, count):
        lo, hi = ROWS[piece]
        place = at_host[src_host[s]][1]
        queue.wait_ge(S["%s%d" % (piece, s)], count)
        queue.dma_start(T.y[lo:hi, place * w:(place + 1) * w], T["l" + piece][s]).then_inc(S.stored, 16)

    g.sync.dma_start(T.sc[:], T.x[80:128, :]).then_inc(S.loaded, 16)
    g.scalar.dma_start(T.sa[:], T.x[0:48, :]).then_inc(S.loaded, 16)
    g.sync.dma_start(T.sb[:], T.x[48:80, :]).then_inc(S.loaded_b, 16)
    g.wait_ge(S.loaded, 32)
    g.remote_dma_fused([xfer(on_chip_of(nc, HS), T.sc[:], T.sc[:], 0x00F0, S.relay_in),
                        xfer(on_chip_of(ns, HCA), T.sa[:], T.sa[:], 0x000F, S.relay_in),
                        xfer(on_chip_of(h, XC), T.sa[:], T.sa[:], 0xFF00, S.relay_in)], local_sem=S.sent)
    g.wait_ge(S.loaded_b, 16)
    g.remote_dma_fused([xfer(on_chip_of(ns, HCB), T.sb[:], T.sb[:], 0x000F, S.relay_in),
                        xfer(on_chip_of(nc, RANK_CORE), T.sb[:], T.lb[1], 0x00F0, S.b1)], local_sem=S.sent)
    rid, pid = topo.addr(on_chip_of(ns, RANK_CORE), core)
    g.remote_dma(T.lc[0], T.sc[:], S.c0, S.sent, pid, rid, 0x000F)
    g.dma_start(T.y[:, at_host[h][1] * w:(at_host[h][1] + 1) * w], T.x[:]).then_inc(S.own, 16)

    store(g.sync, "c", 0, 4)
    store(g.sync, "a", 0, 8)
    store(g.sync, "b", 2, 8)
    store(g.sync, "a", 1, 8)
    store(g.sync, "a", 2, 8)

    store(g.scalar, "b", 0, 8)
    store(g.scalar, "b", 1, 4)
    store(g.scalar, "c", 1, 8)
    store(g.scalar, "c", 2, 8)

    g.wait_ge(S.own, 16)
    g.wait_ge(S.sent, 28)
    g.wait_ge(S.stored, 16 * 9)
